import numpy as np
import ml_dtypes


def mxq(x, axis, fmt="e4m3"):
    dtype, down = {"e4m3": (ml_dtypes.float8_e4m3fn, 7), "e5m2": (ml_dtypes.float8_e5m2, 14)}[fmt]
    v = np.moveaxis(np.asarray(x, np.float32).astype(ml_dtypes.bfloat16).astype(np.float64), axis, -1)
    blocks = v.reshape(v.shape[:-1] + (-1, 32))
    amax = np.abs(blocks).max(-1, keepdims=True)
    byte = np.maximum(np.where(amax > 0, np.frexp(amax)[1] - 1 + 127, 0) - down, 1)
    scale = np.exp2(byte - 127.0)
    codes = (blocks / scale).astype(np.float32).astype(dtype).astype(np.float64)
    return np.moveaxis((codes * scale).reshape(v.shape), -1, axis)


WIDE = False


def mx_kscale(k):
    if not WIDE:
        return np.ones(k)
    levels = np.array([10, -10, 5, -5, 0])
    if k % 512:
        return np.exp2(np.random.permutation(np.resize(levels, k // 32))).repeat(32)
    a = np.empty((k // 512, 16))
    for p in range(k // 512):
        a[p, :8] = np.random.permutation(np.resize(levels, 8))
        for g in range(8):
            far = levels[np.abs(levels - a[p, g]) >= 10]
            a[p, g + 8] = far[np.random.randint(len(far))]
    return np.exp2(a.ravel()).repeat(32)


def f64(x):
    return np.asarray(x).astype(np.float64)


def striped(idx):
    return np.tile(np.asarray(idx).reshape(-1, 16).T, (8, 1)).astype(np.uint16)


def unstriped(offs):
    return offs[:16].T.reshape(-1).astype(np.int64)


E2M1 = np.array([0.0, 0.5, 1.0, 1.5, 2.0, 3.0, 4.0, 6.0, -0.0, -0.5, -1.0, -1.5, -2.0, -3.0, -4.0, -6.0])


def pack_weight(w, fmt):
    k, n = w.shape
    w = f64(np.asarray(w, np.float32).astype(ml_dtypes.bfloat16)).reshape(k // 32, 32, n)
    amax = np.abs(w).max(1)
    if fmt == "e4m3":
        byte = np.frexp(amax)[1] - 1 + 127 - 7
    else:
        mant, ex = np.frexp(amax / 6.0)
        byte = np.where(mant > 0.5, ex, ex - 1) + 127
    byte = np.clip(np.where(amax > 0, byte, 1), 1, 254)
    scaled = (w * np.exp2(127.0 - byte)[:, None, :]).reshape(k, n).astype(np.float32)
    by_word = np.ascontiguousarray(scaled.reshape(k // 512, 128, 4, n).transpose(0, 1, 3, 2))
    if fmt == "e4m3":
        words = by_word.astype(ml_dtypes.float8_e4m3fn).view(np.uint8)
    else:
        c = by_word.astype(ml_dtypes.float4_e2m1fn).view(np.uint8) & 0xF
        words = (c[..., 0::2] | (c[..., 1::2] << 4)).reshape(k // 512, 128, 2 * n)
    return np.ascontiguousarray(words), np.ascontiguousarray(byte.astype(np.uint8).reshape(k // 512, 16, n))


def unpack_weight(words, scales, fmt):
    g, _, n = scales.shape
    words = np.ascontiguousarray(words).reshape(g, 128, n, -1)
    if fmt == "e4m3":
        vals = words.view(ml_dtypes.float8_e4m3fn).astype(np.float64)
    else:
        nib = np.empty((g, 128, n, 4), np.uint8)
        nib[..., 0::2] = words & 0xF
        nib[..., 1::2] = words >> 4
        vals = E2M1[nib]
    vals = vals * np.repeat(np.exp2(scales.astype(np.float64) - 127.0), 8, axis=1)[..., None]
    return vals.transpose(0, 1, 3, 2).reshape(g * 512, n)


def sigmoid(v):
    return 1.0 / (1.0 + np.exp(-v))


def bf(x):
    return np.asarray(x, np.float32).astype(ml_dtypes.bfloat16)


def planes(Y):
    r, m = Y.shape
    b = f64(bf(Y)).reshape(r // 32, 32, m)
    amax = np.abs(b).max(1)
    byte = np.clip(np.where(amax > 0, np.frexp(amax)[1] - 1 + 127 - 7, 1), 1, 254)
    codes = (b * np.exp2(127.0 - byte)[:, None, :]).reshape(r, m).astype(np.float32).astype(ml_dtypes.float8_e4m3fn).view(np.uint8)
    words = codes.reshape(r // 512, 128, 4, m).transpose(0, 1, 3, 2)
    return np.ascontiguousarray(words), np.ascontiguousarray(byte.astype(np.uint8).reshape(r // 512, 16, m))


K, R, F, T, J, M, N = 512, 512, 512, 2048, 512, 512, 64


def setup_inputs():
    n = np.random.standard_normal
    idx = np.random.permutation(T)[:J]
    idx2 = np.random.permutation(J)[:M]
    idx3 = np.random.permutation(M)[:N]
    fk = mx_kscale(K)
    ff = mx_kscale(F)
    tabp = pack_weight(n((K, T)) / fk[:, None], "e2m1")
    return {
        "tab_words": tabp[0],
        "tab_scales": tabp[1],
        "w1": (n((K, R)) * 1 / np.sqrt(K) * fk[:, None]).astype(np.float32),
        "gain": (np.random.uniform(0.5, 1.5, (R, 1))).astype(np.float32),
        "pb": (np.random.uniform(-0.5, 0.5, (1, M))).astype(np.float32),
        "mix": (np.random.uniform(0.7, 2.0, (R, 1))).astype(np.float32),
        "wo": (n((F, R)) * 1 / np.sqrt(F) * ff[:, None]).astype(np.float32),
        "dy": (n((F, N)) / ff[:, None]).astype(np.float32),
        "old": (0.5 * n((R, J))).astype(np.float32),
        "offs": striped(idx),
        "offs2": striped(idx2),
        "offs3": striped(idx3),
    }


def reference(tab_words, tab_scales, w1, gain, pb, mix, wo, dy, old, offs, offs2, offs3):
    idx = unstriped(offs)
    idx2 = unstriped(offs2)
    idx3 = unstriped(offs3)
    tabu = unpack_weight(tab_words, tab_scales, "e2m1")
    w1q = mxq(f64(w1), 0, "e4m3")
    tabidxg = tabu[:, idx]
    a = w1q.T @ tabidxg
    h1 = np.tanh(a)
    h2 = h1 * f64(gain)
    s = h2[:, idx2] + f64(pb)
    v1 = s[:, idx3] * f64(mix)
    woq = mxq(f64(wo), 0, "e4m3")
    dyq = mxq(f64(dy), 0, "e4m3")
    c0 = woq.T @ dyq
    dv1 = c0 * sigmoid(v1) * (1.0 + v1 * (1.0 - sigmoid(v1)))
    e1 = dv1 * f64(mix)
    s1 = np.zeros((R, M))
    s1[:, idx3] = e1
    s2 = np.zeros((R, J))
    s2[:, idx2] = s1
    dh1 = s2 * f64(gain)
    da = dh1 * (1.0 - np.square(h1))
    y = da + f64(old)
    words, scales = planes(y)
    return y, words, scales

@@ -1,0 +1,206 @@
+from contextlib import ExitStack
+
+import concourse.mybir as mybir
+from concourse.masks import make_identity
+
+K, R, F, T, J, M, N = 512, 512, 512, 2048, 512, 512, 64
+FLOPS = 2 * K * R * J + 2 * F * R * N
+
+F32 = mybir.dt.float32
+BF16 = mybir.dt.bfloat16
+I32 = mybir.dt.int32
+U32 = mybir.dt.uint32
+U16 = mybir.dt.uint16
+U8 = mybir.dt.uint8
+FP8X4 = mybir.dt.float8_e4m3fn_x4
+FP4X4 = mybir.dt.float4_e2m1fn_x4
+ACT = mybir.ActivationFunctionType
+ALU = mybir.AluOpType
+
+P = 128
+PACK = 4
+GATHER_SPARE = 16
+SCATTER_SPARE = 192
+HALVES = (slice(0, J // 2), slice(J // 2, J))
+PAIRS = (slice(0, 2), slice(2, 4))
+
+
+def tile_attend_ctwohops_pl_kernel(
+    tc, tab_words, tab_scales, w1, gain, pb, mix, wo, dy, old, offs, offs2, offs3, out_0, out_1, out_2
+):
+    nc = tc.nc
+    with ExitStack() as ctx:
+        sb = ctx.enter_context(tc.tile_pool(name="sb", bufs=1))
+        ps = ctx.enter_context(tc.psum_pool(name="ps", bufs=1))
+
+        def one(name, shape, dtype):
+            return sb.tile(shape, dtype, name=name, align_bytes=64)
+
+        def several(name, count, shape, dtype):
+            return [one("%s%d" % (name, t), shape, dtype) for t in range(count)]
+
+        idx = one("idx", [P, J // 16], U16)
+        idx2 = one("idx2", [P, M // 16], U16)
+        idx3 = one("idx3", [P, N // 16], U16)
+        tabw = one("tabw", [P, T], U16)
+        tabs = one("tabs", [P, T], U8)
+        w1_raw = one("w1_raw", [P, PACK, R], F32)
+        wo_raw = one("wo_raw", [P, PACK, R], F32)
+        dy_raw = one("dy_raw", [P, PACK, N], F32)
+        old_sb = one("old_sb", [P, PACK, J], F32)
+        gain_sb = one("gain_sb", [P, PACK], F32)
+        mix_sb = one("mix_sb", [P, PACK], F32)
+        pb_col = one("pb_col", [P, PACK], F32)
+        ident = one("ident", [P, P], F32)
+        h1 = several("h1", PACK, [P, J], F32)
+        h2 = several("h2", PACK, [P, J + GATHER_SPARE], F32)
+        sq = several("sq", PACK, [P, J], F32)
+        slope = several("slope", PACK, [P, J], F32)
+        s = several("s", PACK, [P, M], F32)
+        s1 = several("s1", PACK, [P, M], F32)
+        s2 = several("s2", PACK, [P, J + SCATTER_SPARE], F32)
+        da = several("da", PACK, [P, J], F32)
+
+        nc.vector.memset(tabs[:].bitcast(I32), 0)
+        nc.sync.dma_start(idx[:], offs)
+        for q in range(4):
+            nc.scalar.dma_start(
+                out=tabs[32 * q : 32 * q + 4, :].bitcast(I32), in_=tab_scales[0, 4 * q : 4 * q + 4, :].bitcast(I32)
+            )
+        nc.sync.dma_start(out=w1_raw[:], in_=w1.rearrange("(p j) r -> p j r", j=PACK))
+        nc.sync.dma_start(out=tabw[:].bitcast(I32), in_=tab_words[0].bitcast(I32))
+        nc.sync.dma_start(out=pb_col[:], in_=pb.rearrange("o (p c) -> p (o c)", c=PACK))
+        nc.sync.dma_start(out=gain_sb[:], in_=gain.rearrange("(p t) o -> p (t o)", t=PACK))
+        nc.sync.dma_start(idx2[:], offs2)
+        nc.sync.dma_start(out=mix_sb[:], in_=mix.rearrange("(p t) o -> p (t o)", t=PACK))
+        nc.sync.dma_start(idx3[:], offs3)
+        nc.sync.dma_start(out=dy_raw[:], in_=dy.rearrange("(p j) n -> p j n", j=PACK))
+        nc.sync.dma_start(out=wo_raw[:], in_=wo.rearrange("(p j) r -> p j r", j=PACK))
+        nc.sync.dma_start(out=old_sb[:], in_=old.rearrange("(p t) j -> p t j", t=PACK))
+        make_identity(nc, ident[:])
+        for t in range(PACK):
+            nc.vector.memset(h2[t][:, J:], 0.0)
+            nc.vector.memset(s1[t][:], 0.0)
+
+        def deal(copy, dealt, raw, pair):
+            copy(
+                out=dealt[:].rearrange("p t m j -> p m j t"),
+                in_=raw[:].rearrange("p j (m t) -> p m j t", t=PACK)[:, :, :, pair],
+            )
+
+        def quantize(codes, scales, values):
+            nc.vector.quantize_mx(out=codes.bitcast(FP8X4), scales=scales, in_=values)
+
+        def product(result, w_codes, w_scales, x_codes, x_scales):
+            nc.tensor.matmul_mx(
+                out=result, lhsT=w_codes.bitcast(FP8X4), lhsT_scale=w_scales, rhs=x_codes, rhs_scale=x_scales,
+                start=True, stop=True,
+            )
+
+        gs = one("gs", [P, J], U8)
+        gw = one("gw", [P, J], U16)
+        nc.vector.tensor_copy(gs[:], tabs[:].indirect(idx[:]))
+        w1_bf = several("w1_bf", 2, [P, 2, P, PACK], BF16)
+        deal(nc.vector.tensor_copy, w1_bf[0], w1_raw, PAIRS[0])
+        deal(nc.scalar.copy, w1_bf[1], w1_raw, PAIRS[1])
+        w1_codes = several("w1_codes", 2, [P, 2 * P], U32)
+        w1_sc = several("w1_sc", 2, [P, 2 * P], U8)
+        quantize(w1_codes[0][:], w1_sc[0][:], w1_bf[0][:].rearrange("p t m j -> p (t m j)"))
+        for h in range(2):
+            nc.vector.tensor_copy(gw[:, HALVES[h]], tabw[:].indirect(idx[:, 16 * h : 16 * (h + 1)]))
+        quantize(w1_codes[1][:], w1_sc[1][:], w1_bf[1][:].rearrange("p t m j -> p (t m j)"))
+
+        pb_ps = ps.tile([P, PACK, P], F32, name="pb_ps")
+        for c in range(PACK):
+            nc.tensor.transpose(pb_ps[:, c, :], pb_col[:, c : c + 1].to_broadcast([P, P]), ident[:])
+        pb_all = one("pb_all", [P, M], F32)
+        nc.scalar.copy(out=pb_all[:].rearrange("x (p c) -> x p c", c=PACK), in_=pb_ps[:].rearrange("x c p -> x p c"))
+
+        mix_all = one("mix_all", [P, PACK, N], F32)
+        v1 = one("v1", [P, PACK, N], F32)
+        for t in range(PACK):
+            w_cols = slice(P * (t % 2), P * (t % 2 + 1))
+            for cols in HALVES if t == 0 else (slice(0, J),):
+                a = ps.tile([P, cols.stop - cols.start], F32, name="a%d_%d" % (t, cols.start))
+                product(
+                    a[:], w1_codes[t // 2][:, w_cols], w1_sc[t // 2][:, w_cols], gw[:, cols].bitcast(FP4X4), gs[:, cols]
+                )
+                nc.scalar.activation(out=h1[t][:, cols], in_=a[:], func=ACT.Tanh)
+                nc.scalar.activation(out=h2[t][:, cols], in_=h1[t][:, cols], func=ACT.Copy, scale=gain_sb[:, t : t + 1])
+            if t == 0:
+                nc.scalar.copy(out=mix_all[:], in_=mix_sb[:].unsqueeze(2).to_broadcast([P, PACK, N]))
+            nc.vector.tensor_tensor(s[t][:], h2[t][:].indirect(idx2[:]), pb_all[:], ALU.add)
+            if t > 0:
+                nc.vector.tensor_tensor(v1[:, t - 1, :], s[t - 1][:].indirect(idx3[:]), mix_all[:, t - 1, :], ALU.mult)
+        nc.vector.tensor_tensor(v1[:, PACK - 1, :], s[PACK - 1][:].indirect(idx3[:]), mix_all[:, PACK - 1, :], ALU.mult)
+
+        dy_bf = one("dy_bf", [P, N, PACK], BF16)
+        nc.scalar.copy(out=dy_bf[:], in_=dy_raw[:].rearrange("p j n -> p n j"))
+        dy_codes = one("dy_codes", [P, N], U32)
+        dy_sc = one("dy_sc", [P, N], U8)
+        quantize(dy_codes[:], dy_sc[:], dy_bf[:].rearrange("p n j -> p (n j)"))
+        wo_bf = several("wo_bf", 2, [P, 2, P, PACK], BF16)
+        wo_codes = several("wo_codes", 2, [P, 2 * P], U32)
+        wo_sc = several("wo_sc", 2, [P, 2 * P], U8)
+        cm = several("cm", 2, [P, 2, N], F32)
+        th = several("th", 2, [P, 2, N], F32)
+        sig = several("sig", 2, [P, 2, N], F32)
+        nsig = several("nsig", 2, [P, 2, N], F32)
+        u = several("u", 2, [P, 2, N], F32)
+        w = several("w", 2, [P, 2, N], F32)
+        for h in range(2):
+            deal(nc.scalar.copy, wo_bf[h], wo_raw, PAIRS[h])
+            quantize(wo_codes[h][:], wo_sc[h][:], wo_bf[h][:].rearrange("p t m j -> p (t m j)"))
+            c0 = ps.tile([P, 2, N], F32, name="c0_%d" % h)
+            for e in range(2):
+                w_cols = slice(P * e, P * (e + 1))
+                product(c0[:, e, :], wo_codes[h][:, w_cols], wo_sc[h][:, w_cols], dy_codes[:].bitcast(FP8X4), dy_sc[:])
+            nc.scalar.activation(out=th[h][:], in_=v1[:, PAIRS[h], :], func=ACT.Tanh, scale=0.5)
+            nc.scalar.activation(out=nsig[h][:], in_=th[h][:], func=ACT.Identity, scale=-0.5, bias=0.5)
+            nc.scalar.activation(out=sig[h][:], in_=th[h][:], func=ACT.Identity, scale=0.5, bias=0.5)
+            for e in range(2):
+                t = 2 * h + e
+                nc.scalar.activation(out=cm[h][:, e, :], in_=c0[:, e, :], func=ACT.Copy, scale=mix_sb[:, t : t + 1])
+            nc.vector.tensor_tensor(u[h][:], nsig[h][:], v1[:, PAIRS[h], :], ALU.mult)
+            nc.vector.scalar_tensor_tensor(w[h][:], u[h][:], 1.0, sig[h][:], ALU.add, ALU.mult)
+            for e in range(2):
+                nc.vector.tensor_tensor(s1[2 * h + e][:].indirect(idx3[:]), w[h][:, e, :], cm[h][:, e, :], ALU.mult)
+
+        neg_gain = one("neg_gain", [P, PACK], F32)
+        nc.scalar.activation(out=neg_gain[:], in_=gain_sb[:], func=ACT.Copy, scale=-1.0)
+        for t in range(PACK):
+            nc.scalar.activation(out=sq[t][:], in_=h1[t][:], func=ACT.Square)
+            nc.scalar.activation(
+                out=slope[t][:], in_=sq[t][:], func=ACT.Identity, scale=neg_gain[:, t : t + 1], bias=gain_sb[:, t : t + 1]
+            )
+
+        y = one("y", [P, PACK, J], F32)
+        out_rows = out_0.rearrange("(p t) j -> p t j", t=PACK)
+        last = PACK - 1
+        for t in range(PACK):
+            nc.vector.tensor_copy(s2[t][:].indirect(idx2[:]), s1[t][:])
+            if t < last:
+                nc.vector.tensor_tensor(da[t][:], s2[t][:, 0:J], slope[t][:], ALU.mult)
+                nc.vector.tensor_tensor(y[:, t, :], da[t][:], old_sb[:, t, :], ALU.add)
+                nc.sync.dma_start(out=out_rows[:, t, :], in_=y[:, t, :])
+        for cols in HALVES:
+            nc.vector.tensor_tensor(da[last][:, cols], s2[last][:, cols], slope[last][:, cols], ALU.mult)
+        for cols in HALVES:
+            nc.vector.tensor_tensor(y[:, last, cols], da[last][:, cols], old_sb[:, last, cols], ALU.add)
+        nc.sync.dma_start(out=out_rows[:, last, :], in_=y[:, last, :])
+
+        y_bf = several("y_bf", 2, [P, J // 2, PACK], BF16)
+        y_codes = one("y_codes", [P, J], U32)
+        y_sc = one("y_sc", [P, J], U8)
+        for h, copy in enumerate((nc.scalar.copy, nc.vector.tensor_copy)):
+            copy(
+                out=y_bf[h][:].rearrange("p (c i) t -> p c t i", i=4),
+                in_=y[:, :, HALVES[h]].rearrange("p t (c i) -> p c t i", i=4),
+            )
+        for h in (1, 0):
+            quantize(y_codes[:, HALVES[h]], y_sc[:, HALVES[h]], y_bf[h][:].rearrange("p j t -> p (j t)"))
+        nc.sync.dma_start(out=out_1[0].rearrange("p c r -> p (c r)").bitcast(I32), in_=y_codes[:].bitcast(I32))
+        for q in range(4):
+            nc.scalar.dma_start(
+                out=out_2[0, 4 * q : 4 * q + 4, :].bitcast(I32), in_=y_sc[32 * q : 32 * q + 4, :].bitcast(I32)
+            )

@@ -44,7 +44,7 @@ def tile_attend_ctwohops_pl_kernel(
         idx3 = one("idx3", [P, N // 16], U16)
         tabw = one("tabw", [P, T], U16)
         tabs = one("tabs", [P, T], U8)
-        w1_raw = one("w1_raw", [P, PACK, R], F32)
+        w1_raw = several("w1_raw", 2, [P, PACK, R // 2], F32)
         wo_raw = one("wo_raw", [P, PACK, R], F32)
         dy_raw = one("dy_raw", [P, PACK, N], F32)
         old_sb = one("old_sb", [P, PACK, J], F32)
@@ -61,21 +61,22 @@ def tile_attend_ctwohops_pl_kernel(
         s2 = several("s2", PACK, [P, J + SCATTER_SPARE], F32)
         da = several("da", PACK, [P, J], F32)
 
-        nc.vector.memset(tabs[:].bitcast(I32), 0)
+        nc.gpsimd.memset(tabs[:].bitcast(I32), 0)
         nc.sync.dma_start(idx[:], offs)
+        nc.sync.dma_start(out=tabw[:].bitcast(I32), in_=tab_words[0].bitcast(I32))
         for q in range(4):
-            nc.scalar.dma_start(
+            nc.sync.dma_start(
                 out=tabs[32 * q : 32 * q + 4, :].bitcast(I32), in_=tab_scales[0, 4 * q : 4 * q + 4, :].bitcast(I32)
             )
-        nc.sync.dma_start(out=w1_raw[:], in_=w1.rearrange("(p j) r -> p j r", j=PACK))
-        nc.sync.dma_start(out=tabw[:].bitcast(I32), in_=tab_words[0].bitcast(I32))
+        for h in range(2):
+            nc.sync.dma_start(out=w1_raw[h][:], in_=w1.rearrange("(p j) r -> p j r", j=PACK)[:, :, HALVES[h]])
         nc.sync.dma_start(out=pb_col[:], in_=pb.rearrange("o (p c) -> p (o c)", c=PACK))
         nc.sync.dma_start(out=gain_sb[:], in_=gain.rearrange("(p t) o -> p (t o)", t=PACK))
         nc.sync.dma_start(idx2[:], offs2)
+        nc.sync.dma_start(out=wo_raw[:], in_=wo.rearrange("(p j) r -> p j r", j=PACK))
+        nc.sync.dma_start(out=dy_raw[:], in_=dy.rearrange("(p j) n -> p j n", j=PACK))
         nc.sync.dma_start(out=mix_sb[:], in_=mix.rearrange("(p t) o -> p (t o)", t=PACK))
         nc.sync.dma_start(idx3[:], offs3)
-        nc.sync.dma_start(out=dy_raw[:], in_=dy.rearrange("(p j) n -> p j n", j=PACK))
-        nc.sync.dma_start(out=wo_raw[:], in_=wo.rearrange("(p j) r -> p j r", j=PACK))
         nc.sync.dma_start(out=old_sb[:], in_=old.rearrange("(p t) j -> p t j", t=PACK))
         make_identity(nc, ident[:])
         for t in range(PACK):
@@ -84,8 +85,8 @@ def tile_attend_ctwohops_pl_kernel(
 
         def deal(copy, dealt, raw, pair):
             copy(
-                out=dealt[:].rearrange("p t m j -> p m j t"),
-                in_=raw[:].rearrange("p j (m t) -> p m j t", t=PACK)[:, :, :, pair],
+                out=dealt.rearrange("p t m j -> p m j t"),
+                in_=raw.rearrange("p j (m t) -> p m j t", t=PACK)[:, :, :, pair],
             )
 
         def quantize(codes, scales, values):
@@ -99,15 +100,18 @@ def tile_attend_ctwohops_pl_kernel(
 
         gs = one("gs", [P, J], U8)
         gw = one("gw", [P, J], U16)
+        nc.vector.tensor_copy(gw[:], tabw[:].indirect(idx[:]))
         nc.vector.tensor_copy(gs[:], tabs[:].indirect(idx[:]))
         w1_bf = several("w1_bf", 2, [P, 2, P, PACK], BF16)
-        deal(nc.vector.tensor_copy, w1_bf[0], w1_raw, PAIRS[0])
-        deal(nc.scalar.copy, w1_bf[1], w1_raw, PAIRS[1])
+        deal(nc.scalar.copy, w1_bf[0][:, :, 0 : P // 2, :], w1_raw[0][:], PAIRS[0])
+        deal(nc.vector.tensor_copy, w1_bf[0][:, :, P // 2 : P, :], w1_raw[1][:], PAIRS[0])
+        deal(nc.scalar.copy, w1_bf[1][:, :, 0 : P // 2, :], w1_raw[0][:], PAIRS[1])
+        deal(nc.scalar.copy, w1_bf[1][:, :, P // 2 : P, :], w1_raw[1][:], PAIRS[1])
         w1_codes = several("w1_codes", 2, [P, 2 * P], U32)
         w1_sc = several("w1_sc", 2, [P, 2 * P], U8)
-        quantize(w1_codes[0][:], w1_sc[0][:], w1_bf[0][:].rearrange("p t m j -> p (t m j)"))
-        for h in range(2):
-            nc.vector.tensor_copy(gw[:, HALVES[h]], tabw[:].indirect(idx[:, 16 * h : 16 * (h + 1)]))
+        for e in range(2):
+            w_cols = slice(P * e, P * (e + 1))
+            quantize(w1_codes[0][:, w_cols], w1_sc[0][:, w_cols], w1_bf[0][:, e].rearrange("p m j -> p (m j)"))
         quantize(w1_codes[1][:], w1_sc[1][:], w1_bf[1][:].rearrange("p t m j -> p (t m j)"))
 
         pb_ps = ps.tile([P, PACK, P], F32, name="pb_ps")
@@ -149,7 +153,7 @@ def tile_attend_ctwohops_pl_kernel(
         u = several("u", 2, [P, 2, N], F32)
         w = several("w", 2, [P, 2, N], F32)
         for h in range(2):
-            deal(nc.scalar.copy, wo_bf[h], wo_raw, PAIRS[h])
+            deal(nc.scalar.copy, wo_bf[h][:], wo_raw[:], PAIRS[h])
             quantize(wo_codes[h][:], wo_sc[h][:], wo_bf[h][:].rearrange("p t m j -> p (t m j)"))
             c0 = ps.tile([P, 2, N], F32, name="c0_%d" % h)
             for e in range(2):
@@ -180,8 +184,8 @@ def tile_attend_ctwohops_pl_kernel(
         for t in range(PACK):
             nc.vector.tensor_copy(s2[t][:].indirect(idx2[:]), s1[t][:])
             if t < last:
-                nc.vector.tensor_tensor(da[t][:], s2[t][:, 0:J], slope[t][:], ALU.mult)
-                nc.vector.tensor_tensor(y[:, t, :], da[t][:], old_sb[:, t, :], ALU.add)
+                nc.gpsimd.tensor_tensor(da[t][:], s2[t][:, 0:J], slope[t][:], ALU.mult)
+                nc.gpsimd.tensor_tensor(y[:, t, :], da[t][:], old_sb[:, t, :], ALU.add)
                 nc.sync.dma_start(out=out_rows[:, t, :], in_=y[:, t, :])
         for cols in HALVES:
             nc.vector.tensor_tensor(da[last][:, cols], s2[last][:, cols], slope[last][:, cols], ALU.mult)

@@ -58,11 +58,11 @@ def tile_attend_ctwohops_pl_kernel(
         slope = several("slope", PACK, [P, J], F32)
         s = several("s", PACK, [P, M], F32)
         s1 = several("s1", PACK, [P, M], F32)
-        s2 = several("s2", PACK, [P, J + SCATTER_SPARE], F32)
-        da = several("da", PACK, [P, J], F32)
+        da = [sb.tile([P, J], F32, name="da%d" % t, tag="da%d" % (t // 3), align_bytes=64) for t in range(PACK)]
 
         nc.gpsimd.memset(tabs[:].bitcast(I32), 0)
         nc.sync.dma_start(idx[:], offs)
+        nc.sync.dma_start(out=pb_col[:], in_=pb.rearrange("o (p c) -> p (o c)", c=PACK))
         nc.sync.dma_start(out=tabw[:].bitcast(I32), in_=tab_words[0].bitcast(I32))
         for q in range(4):
             nc.sync.dma_start(
@@ -70,12 +70,11 @@ def tile_attend_ctwohops_pl_kernel(
             )
         for h in range(2):
             nc.sync.dma_start(out=w1_raw[h][:], in_=w1.rearrange("(p j) r -> p j r", j=PACK)[:, :, HALVES[h]])
-        nc.sync.dma_start(out=pb_col[:], in_=pb.rearrange("o (p c) -> p (o c)", c=PACK))
         nc.sync.dma_start(out=gain_sb[:], in_=gain.rearrange("(p t) o -> p (t o)", t=PACK))
         nc.sync.dma_start(idx2[:], offs2)
+        nc.sync.dma_start(out=mix_sb[:], in_=mix.rearrange("(p t) o -> p (t o)", t=PACK))
         nc.sync.dma_start(out=wo_raw[:], in_=wo.rearrange("(p j) r -> p j r", j=PACK))
         nc.sync.dma_start(out=dy_raw[:], in_=dy.rearrange("(p j) n -> p j n", j=PACK))
-        nc.sync.dma_start(out=mix_sb[:], in_=mix.rearrange("(p t) o -> p (t o)", t=PACK))
         nc.sync.dma_start(idx3[:], offs3)
         nc.sync.dma_start(out=old_sb[:], in_=old.rearrange("(p t) j -> p t j", t=PACK))
         make_identity(nc, ident[:])
@@ -130,7 +129,12 @@ def tile_attend_ctwohops_pl_kernel(
                     a[:], w1_codes[t // 2][:, w_cols], w1_sc[t // 2][:, w_cols], gw[:, cols].bitcast(FP4X4), gs[:, cols]
                 )
                 nc.scalar.activation(out=h1[t][:, cols], in_=a[:], func=ACT.Tanh)
-                nc.scalar.activation(out=h2[t][:, cols], in_=h1[t][:, cols], func=ACT.Copy, scale=gain_sb[:, t : t + 1])
+                if t == 0:
+                    nc.vector.tensor_scalar_mul(h2[t][:, cols], h1[t][:, cols], gain_sb[:, t : t + 1])
+                else:
+                    nc.scalar.activation(
+                        out=h2[t][:, cols], in_=h1[t][:, cols], func=ACT.Copy, scale=gain_sb[:, t : t + 1]
+                    )
             if t == 0:
                 nc.scalar.copy(out=mix_all[:], in_=mix_sb[:].unsqueeze(2).to_broadcast([P, PACK, N]))
             nc.vector.tensor_tensor(s[t][:], h2[t][:].indirect(idx2[:]), pb_all[:], ALU.add)
@@ -146,7 +150,10 @@ def tile_attend_ctwohops_pl_kernel(
         wo_bf = several("wo_bf", 2, [P, 2, P, PACK], BF16)
         wo_codes = several("wo_codes", 2, [P, 2 * P], U32)
         wo_sc = several("wo_sc", 2, [P, 2 * P], U8)
-        cm = several("cm", 2, [P, 2, N], F32)
+        c0 = ps.tile([P, PACK, N], F32, name="c0")
+        c0_sb = one("c0_sb", [P, PACK, N], F32)
+        half_mix = one("half_mix", [P, PACK], F32)
+        nc.scalar.activation(out=half_mix[:], in_=mix_sb[:], func=ACT.Copy, scale=0.5)
         th = several("th", 2, [P, 2, N], F32)
         sig = several("sig", 2, [P, 2, N], F32)
         nsig = several("nsig", 2, [P, 2, N], F32)
@@ -155,20 +162,22 @@ def tile_attend_ctwohops_pl_kernel(
         for h in range(2):
             deal(nc.scalar.copy, wo_bf[h][:], wo_raw[:], PAIRS[h])
             quantize(wo_codes[h][:], wo_sc[h][:], wo_bf[h][:].rearrange("p t m j -> p (t m j)"))
-            c0 = ps.tile([P, 2, N], F32, name="c0_%d" % h)
             for e in range(2):
                 w_cols = slice(P * e, P * (e + 1))
-                product(c0[:, e, :], wo_codes[h][:, w_cols], wo_sc[h][:, w_cols], dy_codes[:].bitcast(FP8X4), dy_sc[:])
+                product(
+                    c0[:, 2 * h + e, :], wo_codes[h][:, w_cols], wo_sc[h][:, w_cols], dy_codes[:].bitcast(FP8X4), dy_sc[:]
+                )
+        for h in range(2):
             nc.scalar.activation(out=th[h][:], in_=v1[:, PAIRS[h], :], func=ACT.Tanh, scale=0.5)
             nc.scalar.activation(out=nsig[h][:], in_=th[h][:], func=ACT.Identity, scale=-0.5, bias=0.5)
-            nc.scalar.activation(out=sig[h][:], in_=th[h][:], func=ACT.Identity, scale=0.5, bias=0.5)
             for e in range(2):
-                t = 2 * h + e
-                nc.scalar.activation(out=cm[h][:, e, :], in_=c0[:, e, :], func=ACT.Copy, scale=mix_sb[:, t : t + 1])
+                factor = half_mix[:, 2 * h + e : 2 * h + e + 1]
+                nc.scalar.activation(out=sig[h][:, e, :], in_=th[h][:, e, :], func=ACT.Identity, scale=factor, bias=factor)
             nc.vector.tensor_tensor(u[h][:], nsig[h][:], v1[:, PAIRS[h], :], ALU.mult)
             nc.vector.scalar_tensor_tensor(w[h][:], u[h][:], 1.0, sig[h][:], ALU.add, ALU.mult)
-            for e in range(2):
-                nc.vector.tensor_tensor(s1[2 * h + e][:].indirect(idx3[:]), w[h][:, e, :], cm[h][:, e, :], ALU.mult)
+        nc.scalar.copy(out=c0_sb[:], in_=c0[:])
+        for t in range(PACK):
+            nc.vector.tensor_tensor(s1[t][:].indirect(idx3[:]), w[t // 2][:, t % 2, :], c0_sb[:, t, :], ALU.mult)
 
         neg_gain = one("neg_gain", [P, PACK], F32)
         nc.scalar.activation(out=neg_gain[:], in_=gain_sb[:], func=ACT.Copy, scale=-1.0)
@@ -181,6 +190,7 @@ def tile_attend_ctwohops_pl_kernel(
         y = one("y", [P, PACK, J], F32)
         out_rows = out_0.rearrange("(p t) j -> p t j", t=PACK)
         last = PACK - 1
+        s2 = several("s2", PACK, [P, J + SCATTER_SPARE], F32)
         for t in range(PACK):
             nc.vector.tensor_copy(s2[t][:].indirect(idx2[:]), s1[t][:])
             if t < last:
@@ -196,15 +206,22 @@ def tile_attend_ctwohops_pl_kernel(
         y_bf = several("y_bf", 2, [P, J // 2, PACK], BF16)
         y_codes = one("y_codes", [P, J], U32)
         y_sc = one("y_sc", [P, J], U8)
-        for h, copy in enumerate((nc.scalar.copy, nc.vector.tensor_copy)):
+        def round_pair(copy, h, pair):
             copy(
-                out=y_bf[h][:].rearrange("p (c i) t -> p c t i", i=4),
-                in_=y[:, :, HALVES[h]].rearrange("p t (c i) -> p c t i", i=4),
+                out=y_bf[h][:].rearrange("p (c i) t -> p c t i", i=4)[:, :, pair, :],
+                in_=y[:, :, HALVES[h]].rearrange("p t (c i) -> p c t i", i=4)[:, :, pair, :],
             )
-        for h in (1, 0):
+
+        for h in range(2):
+            round_pair(nc.scalar.copy, h, PAIRS[0])
+        round_pair(nc.scalar.copy, 0, PAIRS[1])
+        round_pair(nc.vector.tensor_copy, 1, PAIRS[1])
+        words = out_1[0].rearrange("p c r -> p (c r)").bitcast(I32)
+        for h in range(2):
             quantize(y_codes[:, HALVES[h]], y_sc[:, HALVES[h]], y_bf[h][:].rearrange("p j t -> p (j t)"))
-        nc.sync.dma_start(out=out_1[0].rearrange("p c r -> p (c r)").bitcast(I32), in_=y_codes[:].bitcast(I32))
+            nc.sync.dma_start(out=words[:, HALVES[h]], in_=y_codes[:, HALVES[h]].bitcast(I32))
         for q in range(4):
-            nc.scalar.dma_start(
+            queue = nc.scalar if q % 2 == 0 else nc.sync
+            queue.dma_start(
                 out=out_2[0, 4 * q : 4 * q + 4, :].bitcast(I32), in_=y_sc[32 * q : 32 * q + 4, :].bitcast(I32)
             )

@@ -61,26 +61,27 @@ def tile_attend_ctwohops_pl_kernel(
         da = [sb.tile([P, J], F32, name="da%d" % t, tag="da%d" % (t // 3), align_bytes=64) for t in range(PACK)]
 
         nc.gpsimd.memset(tabs[:].bitcast(I32), 0)
-        nc.sync.dma_start(idx[:], offs)
-        nc.sync.dma_start(out=pb_col[:], in_=pb.rearrange("o (p c) -> p (o c)", c=PACK))
         nc.sync.dma_start(out=tabw[:].bitcast(I32), in_=tab_words[0].bitcast(I32))
+        nc.sync.dma_start(idx[:], offs)
         for q in range(4):
             nc.sync.dma_start(
                 out=tabs[32 * q : 32 * q + 4, :].bitcast(I32), in_=tab_scales[0, 4 * q : 4 * q + 4, :].bitcast(I32)
             )
         for h in range(2):
             nc.sync.dma_start(out=w1_raw[h][:], in_=w1.rearrange("(p j) r -> p j r", j=PACK)[:, :, HALVES[h]])
+        nc.sync.dma_start(out=pb_col[:], in_=pb.rearrange("o (p c) -> p (o c)", c=PACK))
         nc.sync.dma_start(out=gain_sb[:], in_=gain.rearrange("(p t) o -> p (t o)", t=PACK))
         nc.sync.dma_start(idx2[:], offs2)
-        nc.sync.dma_start(out=mix_sb[:], in_=mix.rearrange("(p t) o -> p (t o)", t=PACK))
         nc.sync.dma_start(out=wo_raw[:], in_=wo.rearrange("(p j) r -> p j r", j=PACK))
+        nc.sync.dma_start(out=mix_sb[:], in_=mix.rearrange("(p t) o -> p (t o)", t=PACK))
         nc.sync.dma_start(out=dy_raw[:], in_=dy.rearrange("(p j) n -> p j n", j=PACK))
         nc.sync.dma_start(idx3[:], offs3)
         nc.sync.dma_start(out=old_sb[:], in_=old.rearrange("(p t) j -> p t j", t=PACK))
         make_identity(nc, ident[:])
         for t in range(PACK):
-            nc.vector.memset(h2[t][:, J:], 0.0)
-            nc.vector.memset(s1[t][:], 0.0)
+            nc.gpsimd.memset(h2[t][:, J:], 0.0)
+        for t in range(PACK):
+            nc.gpsimd.memset(s1[t][:], 0.0)
 
         def deal(copy, dealt, raw, pair):
             copy(
@@ -101,17 +102,15 @@ def tile_attend_ctwohops_pl_kernel(
         gw = one("gw", [P, J], U16)
         nc.vector.tensor_copy(gw[:], tabw[:].indirect(idx[:]))
         nc.vector.tensor_copy(gs[:], tabs[:].indirect(idx[:]))
-        w1_bf = several("w1_bf", 2, [P, 2, P, PACK], BF16)
-        deal(nc.scalar.copy, w1_bf[0][:, :, 0 : P // 2, :], w1_raw[0][:], PAIRS[0])
-        deal(nc.vector.tensor_copy, w1_bf[0][:, :, P // 2 : P, :], w1_raw[1][:], PAIRS[0])
-        deal(nc.scalar.copy, w1_bf[1][:, :, 0 : P // 2, :], w1_raw[0][:], PAIRS[1])
-        deal(nc.scalar.copy, w1_bf[1][:, :, P // 2 : P, :], w1_raw[1][:], PAIRS[1])
         w1_codes = several("w1_codes", 2, [P, 2 * P], U32)
         w1_sc = several("w1_sc", 2, [P, 2 * P], U8)
-        for e in range(2):
-            w_cols = slice(P * e, P * (e + 1))
-            quantize(w1_codes[0][:, w_cols], w1_sc[0][:, w_cols], w1_bf[0][:, e].rearrange("p m j -> p (m j)"))
-        quantize(w1_codes[1][:], w1_sc[1][:], w1_bf[1][:].rearrange("p t m j -> p (t m j)"))
+        for h, copy in enumerate((nc.scalar.copy, nc.vector.tensor_copy)):
+            w1_bf = one("w1_bf", [P, 2, P, PACK], BF16)
+            for c in range(2):
+                deal(copy, w1_bf[:, :, c * P // 2 : (c + 1) * P // 2, :], w1_raw[c][:], PAIRS[h])
+            for e in range(2):
+                w_cols = slice(P * e, P * (e + 1))
+                quantize(w1_codes[h][:, w_cols], w1_sc[h][:, w_cols], w1_bf[:, e].rearrange("p m j -> p (m j)"))
 
         pb_ps = ps.tile([P, PACK, P], F32, name="pb_ps")
         for c in range(PACK):

from contextlib import ExitStack

import concourse.mybir as mybir
from concourse.masks import make_identity

K, R, F, T, J, M, N = 512, 512, 512, 2048, 512, 512, 64
FLOPS = 2 * K * R * J + 2 * F * R * N

F32 = mybir.dt.float32
BF16 = mybir.dt.bfloat16
I32 = mybir.dt.int32
U32 = mybir.dt.uint32
U16 = mybir.dt.uint16
U8 = mybir.dt.uint8
FP8X4 = mybir.dt.float8_e4m3fn_x4
FP4X4 = mybir.dt.float4_e2m1fn_x4
ACT = mybir.ActivationFunctionType
ALU = mybir.AluOpType

P = 128
PACK = 4
GATHER_SPARE = 16
SCATTER_SPARE = 192
HALVES = (slice(0, J // 2), slice(J // 2, J))
PAIRS = (slice(0, 2), slice(2, 4))


def tile_attend_ctwohops_pl_kernel(
    tc, tab_words, tab_scales, w1, gain, pb, mix, wo, dy, old, offs, offs2, offs3, out_0, out_1, out_2
):
    nc = tc.nc
    with ExitStack() as ctx:
        sb = ctx.enter_context(tc.tile_pool(name="sb", bufs=1))
        ps = ctx.enter_context(tc.psum_pool(name="ps", bufs=1))

        def one(name, shape, dtype):
            return sb.tile(shape, dtype, name=name, align_bytes=64)

        def several(name, count, shape, dtype):
            return [one("%s%d" % (name, t), shape, dtype) for t in range(count)]

        idx = one("idx", [P, J // 16], U16)
        idx2 = one("idx2", [P, M // 16], U16)
        idx3 = one("idx3", [P, N // 16], U16)
        tabw = one("tabw", [P, T], U16)
        tabs = one("tabs", [P, T], U8)
        w1_raw = several("w1_raw", 2, [P, PACK, R // 2], F32)
        wo_raw = one("wo_raw", [P, PACK, R], F32)
        dy_raw = one("dy_raw", [P, PACK, N], F32)
        old_sb = one("old_sb", [P, PACK, J], F32)
        gain_sb = one("gain_sb", [P, PACK], F32)
        mix_sb = one("mix_sb", [P, PACK], F32)
        pb_col = one("pb_col", [P, PACK], F32)
        ident = one("ident", [P, P], F32)
        h1 = several("h1", PACK, [P, J], F32)
        h2 = several("h2", PACK, [P, J + GATHER_SPARE], F32)
        sq = several("sq", PACK, [P, J], F32)
        slope = several("slope", PACK, [P, J], F32)
        s = several("s", PACK, [P, M], F32)
        s1 = several("s1", PACK, [P, M], F32)
        da = [sb.tile([P, J], F32, name="da%d" % t, tag="da%d" % (t // 3), align_bytes=64) for t in range(PACK)]

        nc.gpsimd.memset(tabs[:].bitcast(I32), 0)
        nc.sync.dma_start(out=tabw[:].bitcast(I32), in_=tab_words[0].bitcast(I32))
        nc.sync.dma_start(idx[:], offs)
        for q in range(4):
            nc.sync.dma_start(
                out=tabs[32 * q : 32 * q + 4, :].bitcast(I32), in_=tab_scales[0, 4 * q : 4 * q + 4, :].bitcast(I32)
            )
        for h in range(2):
            nc.sync.dma_start(out=w1_raw[h][:], in_=w1.rearrange("(p j) r -> p j r", j=PACK)[:, :, HALVES[h]])
        nc.sync.dma_start(out=pb_col[:], in_=pb.rearrange("o (p c) -> p (o c)", c=PACK))
        nc.sync.dma_start(out=gain_sb[:], in_=gain.rearrange("(p t) o -> p (t o)", t=PACK))
        nc.sync.dma_start(idx2[:], offs2)
        nc.sync.dma_start(out=wo_raw[:], in_=wo.rearrange("(p j) r -> p j r", j=PACK))
        nc.sync.dma_start(out=mix_sb[:], in_=mix.rearrange("(p t) o -> p (t o)", t=PACK))
        nc.sync.dma_start(out=dy_raw[:], in_=dy.rearrange("(p j) n -> p j n", j=PACK))
        nc.sync.dma_start(idx3[:], offs3)
        nc.sync.dma_start(out=old_sb[:], in_=old.rearrange("(p t) j -> p t j", t=PACK))
        make_identity(nc, ident[:])
        for t in range(PACK):
            nc.gpsimd.memset(h2[t][:, J:], 0.0)
        for t in range(PACK):
            nc.gpsimd.memset(s1[t][:], 0.0)

        def deal(copy, dealt, raw, pair):
            copy(
                out=dealt.rearrange("p t m j -> p m j t"),
                in_=raw.rearrange("p j (m t) -> p m j t", t=PACK)[:, :, :, pair],
            )

        def quantize(codes, scales, values):
            nc.vector.quantize_mx(out=codes.bitcast(FP8X4), scales=scales, in_=values)

        def product(result, w_codes, w_scales, x_codes, x_scales):
            nc.tensor.matmul_mx(
                out=result, lhsT=w_codes.bitcast(FP8X4), lhsT_scale=w_scales, rhs=x_codes, rhs_scale=x_scales,
                start=True, stop=True,
            )

        gs = one("gs", [P, J], U8)
        gw = one("gw", [P, J], U16)
        nc.vector.tensor_copy(gw[:], tabw[:].indirect(idx[:]))
        nc.vector.tensor_copy(gs[:], tabs[:].indirect(idx[:]))
        w1_codes = several("w1_codes", 2, [P, 2 * P], U32)
        w1_sc = several("w1_sc", 2, [P, 2 * P], U8)
        for h, copy in enumerate((nc.scalar.copy, nc.vector.tensor_copy)):
            w1_bf = one("w1_bf", [P, 2, P, PACK], BF16)
            for c in range(2):
                deal(copy, w1_bf[:, :, c * P // 2 : (c + 1) * P // 2, :], w1_raw[c][:], PAIRS[h])
            for e in range(2):
                w_cols = slice(P * e, P * (e + 1))
                quantize(w1_codes[h][:, w_cols], w1_sc[h][:, w_cols], w1_bf[:, e].rearrange("p m j -> p (m j)"))

        pb_ps = ps.tile([P, PACK, P], F32, name="pb_ps")
        for c in range(PACK):
            nc.tensor.transpose(pb_ps[:, c, :], pb_col[:, c : c + 1].to_broadcast([P, P]), ident[:])
        pb_all = one("pb_all", [P, M], F32)
        nc.scalar.copy(out=pb_all[:].rearrange("x (p c) -> x p c", c=PACK), in_=pb_ps[:].rearrange("x c p -> x p c"))

        mix_all = one("mix_all", [P, PACK, N], F32)
        v1 = one("v1", [P, PACK, N], F32)
        for t in range(PACK):
            w_cols = slice(P * (t % 2), P * (t % 2 + 1))
            for cols in HALVES if t == 0 else (slice(0, J),):
                a = ps.tile([P, cols.stop - cols.start], F32, name="a%d_%d" % (t, cols.start))
                product(
                    a[:], w1_codes[t // 2][:, w_cols], w1_sc[t // 2][:, w_cols], gw[:, cols].bitcast(FP4X4), gs[:, cols]
                )
                nc.scalar.activation(out=h1[t][:, cols], in_=a[:], func=ACT.Tanh)
                if t == 0:
                    nc.vector.tensor_scalar_mul(h2[t][:, cols], h1[t][:, cols], gain_sb[:, t : t + 1])
                else:
                    nc.scalar.activation(
                        out=h2[t][:, cols], in_=h1[t][:, cols], func=ACT.Copy, scale=gain_sb[:, t : t + 1]
                    )
            if t == 0:
                nc.scalar.copy(out=mix_all[:], in_=mix_sb[:].unsqueeze(2).to_broadcast([P, PACK, N]))
            nc.vector.tensor_tensor(s[t][:], h2[t][:].indirect(idx2[:]), pb_all[:], ALU.add)
            if t > 0:
                nc.vector.tensor_tensor(v1[:, t - 1, :], s[t - 1][:].indirect(idx3[:]), mix_all[:, t - 1, :], ALU.mult)
        nc.vector.tensor_tensor(v1[:, PACK - 1, :], s[PACK - 1][:].indirect(idx3[:]), mix_all[:, PACK - 1, :], ALU.mult)

        dy_bf = one("dy_bf", [P, N, PACK], BF16)
        nc.scalar.copy(out=dy_bf[:], in_=dy_raw[:].rearrange("p j n -> p n j"))
        dy_codes = one("dy_codes", [P, N], U32)
        dy_sc = one("dy_sc", [P, N], U8)
        quantize(dy_codes[:], dy_sc[:], dy_bf[:].rearrange("p n j -> p (n j)"))
        wo_bf = several("wo_bf", 2, [P, 2, P, PACK], BF16)
        wo_codes = several("wo_codes", 2, [P, 2 * P], U32)
        wo_sc = several("wo_sc", 2, [P, 2 * P], U8)
        c0 = ps.tile([P, PACK, N], F32, name="c0")
        c0_sb = one("c0_sb", [P, PACK, N], F32)
        half_mix = one("half_mix", [P, PACK], F32)
        nc.scalar.activation(out=half_mix[:], in_=mix_sb[:], func=ACT.Copy, scale=0.5)
        th = several("th", 2, [P, 2, N], F32)
        sig = several("sig", 2, [P, 2, N], F32)
        nsig = several("nsig", 2, [P, 2, N], F32)
        u = several("u", 2, [P, 2, N], F32)
        w = several("w", 2, [P, 2, N], F32)
        for h in range(2):
            deal(nc.scalar.copy, wo_bf[h][:], wo_raw[:], PAIRS[h])
            quantize(wo_codes[h][:], wo_sc[h][:], wo_bf[h][:].rearrange("p t m j -> p (t m j)"))
            for e in range(2):
                w_cols = slice(P * e, P * (e + 1))
                product(
                    c0[:, 2 * h + e, :], wo_codes[h][:, w_cols], wo_sc[h][:, w_cols], dy_codes[:].bitcast(FP8X4), dy_sc[:]
                )
        for h in range(2):
            nc.scalar.activation(out=th[h][:], in_=v1[:, PAIRS[h], :], func=ACT.Tanh, scale=0.5)
            nc.scalar.activation(out=nsig[h][:], in_=th[h][:], func=ACT.Identity, scale=-0.5, bias=0.5)
            for e in range(2):
                factor = half_mix[:, 2 * h + e : 2 * h + e + 1]
                nc.scalar.activation(out=sig[h][:, e, :], in_=th[h][:, e, :], func=ACT.Identity, scale=factor, bias=factor)
            nc.vector.tensor_tensor(u[h][:], nsig[h][:], v1[:, PAIRS[h], :], ALU.mult)
            nc.vector.scalar_tensor_tensor(w[h][:], u[h][:], 1.0, sig[h][:], ALU.add, ALU.mult)
        nc.scalar.copy(out=c0_sb[:], in_=c0[:])
        for t in range(PACK):
            nc.vector.tensor_tensor(s1[t][:].indirect(idx3[:]), w[t // 2][:, t % 2, :], c0_sb[:, t, :], ALU.mult)

        neg_gain = one("neg_gain", [P, PACK], F32)
        nc.scalar.activation(out=neg_gain[:], in_=gain_sb[:], func=ACT.Copy, scale=-1.0)
        for t in range(PACK):
            nc.scalar.activation(out=sq[t][:], in_=h1[t][:], func=ACT.Square)
            nc.scalar.activation(
                out=slope[t][:], in_=sq[t][:], func=ACT.Identity, scale=neg_gain[:, t : t + 1], bias=gain_sb[:, t : t + 1]
            )

        y = one("y", [P, PACK, J], F32)
        out_rows = out_0.rearrange("(p t) j -> p t j", t=PACK)
        last = PACK - 1
        s2 = several("s2", PACK, [P, J + SCATTER_SPARE], F32)
        for t in range(PACK):
            nc.vector.tensor_copy(s2[t][:].indirect(idx2[:]), s1[t][:])
            if t < last:
                nc.gpsimd.tensor_tensor(da[t][:], s2[t][:, 0:J], slope[t][:], ALU.mult)
                nc.gpsimd.tensor_tensor(y[:, t, :], da[t][:], old_sb[:, t, :], ALU.add)
                nc.sync.dma_start(out=out_rows[:, t, :], in_=y[:, t, :])
        for cols in HALVES:
            nc.vector.tensor_tensor(da[last][:, cols], s2[last][:, cols], slope[last][:, cols], ALU.mult)
        for cols in HALVES:
            nc.vector.tensor_tensor(y[:, last, cols], da[last][:, cols], old_sb[:, last, cols], ALU.add)
        nc.sync.dma_start(out=out_rows[:, last, :], in_=y[:, last, :])

        y_bf = several("y_bf", 2, [P, J // 2, PACK], BF16)
        y_codes = one("y_codes", [P, J], U32)
        y_sc = one("y_sc", [P, J], U8)
        def round_pair(copy, h, pair):
            copy(
                out=y_bf[h][:].rearrange("p (c i) t -> p c t i", i=4)[:, :, pair, :],
                in_=y[:, :, HALVES[h]].rearrange("p t (c i) -> p c t i", i=4)[:, :, pair, :],
            )

        for h in range(2):
            round_pair(nc.scalar.copy, h, PAIRS[0])
        round_pair(nc.scalar.copy, 0, PAIRS[1])
        round_pair(nc.vector.tensor_copy, 1, PAIRS[1])
        words = out_1[0].rearrange("p c r -> p (c r)").bitcast(I32)
        for h in range(2):
            quantize(y_codes[:, HALVES[h]], y_sc[:, HALVES[h]], y_bf[h][:].rearrange("p j t -> p (j t)"))
            nc.sync.dma_start(out=words[:, HALVES[h]], in_=y_codes[:, HALVES[h]].bitcast(I32))
        for q in range(4):
            queue = nc.scalar if q % 2 == 0 else nc.sync
            queue.dma_start(
                out=out_2[0, 4 * q : 4 * q + 4, :].bitcast(I32), in_=y_sc[32 * q : 32 * q + 4, :].bitcast(I32)
            )
